import numpy as np
import ml_dtypes


def mxq(x, axis, fmt="e4m3"):
    dtype, down = {"e4m3": (ml_dtypes.float8_e4m3fn, 7), "e5m2": (ml_dtypes.float8_e5m2, 14)}[fmt]
    v = np.moveaxis(np.asarray(x, np.float32).astype(ml_dtypes.bfloat16).astype(np.float64), axis, -1)
    blocks = v.reshape(v.shape[:-1] + (-1, 32))
    amax = np.abs(blocks).max(-1, keepdims=True)
    byte = np.maximum(np.where(amax > 0, np.frexp(amax)[1] - 1 + 127, 0) - down, 1)
    scale = np.exp2(byte - 127.0)
    codes = (blocks / scale).astype(np.float32).astype(dtype).astype(np.float64)
    return np.moveaxis((codes * scale).reshape(v.shape), -1, axis)


WIDE = False


def mx_kscale(k):
    if not WIDE:
        return np.ones(k)
    levels = np.array([10, -10, 5, -5, 0])
    if k % 512:
        return np.exp2(np.random.permutation(np.resize(levels, k // 32))).repeat(32)
    a = np.empty((k // 512, 16))
    for p in range(k // 512):
        a[p, :8] = np.random.permutation(np.resize(levels, 8))
        for g in range(8):
            far = levels[np.abs(levels - a[p, g]) >= 10]
            a[p, g + 8] = far[np.random.randint(len(far))]
    return np.exp2(a.ravel()).repeat(32)


def f64(x):
    return np.asarray(x).astype(np.float64)


def striped(idx):
    return np.tile(np.asarray(idx).reshape(-1, 16).T, (8, 1)).astype(np.uint16)


def unstriped(offs):
    return offs[:16].T.reshape(-1).astype(np.int64)


E2M1 = np.array([0.0, 0.5, 1.0, 1.5, 2.0, 3.0, 4.0, 6.0, -0.0, -0.5, -1.0, -1.5, -2.0, -3.0, -4.0, -6.0])


def pack_weight(w, fmt):
    k, n = w.shape
    w = f64(np.asarray(w, np.float32).astype(ml_dtypes.bfloat16)).reshape(k // 32, 32, n)
    amax = np.abs(w).max(1)
    if fmt == "e4m3":
        byte = np.frexp(amax)[1] - 1 + 127 - 7
    else:
        mant, ex = np.frexp(amax / 6.0)
        byte = np.where(mant > 0.5, ex, ex - 1) + 127
    byte = np.clip(np.where(amax > 0, byte, 1), 1, 254)
    scaled = (w * np.exp2(127.0 - byte)[:, None, :]).reshape(k, n).astype(np.float32)
    by_word = np.ascontiguousarray(scaled.reshape(k // 512, 128, 4, n).transpose(0, 1, 3, 2))
    if fmt == "e4m3":
        words = by_word.astype(ml_dtypes.float8_e4m3fn).view(np.uint8)
    else:
        c = by_word.astype(ml_dtypes.float4_e2m1fn).view(np.uint8) & 0xF
        words = (c[..., 0::2] | (c[..., 1::2] << 4)).reshape(k // 512, 128, 2 * n)
    return np.ascontiguousarray(words), np.ascontiguousarray(byte.astype(np.uint8).reshape(k // 512, 16, n))


def unpack_weight(words, scales, fmt):
    g, _, n = scales.shape
    words = np.ascontiguousarray(words).reshape(g, 128, n, -1)
    if fmt == "e4m3":
        vals = words.view(ml_dtypes.float8_e4m3fn).astype(np.float64)
    else:
        nib = np.empty((g, 128, n, 4), np.uint8)
        nib[..., 0::2] = words & 0xF
        nib[..., 1::2] = words >> 4
        vals = E2M1[nib]
    vals = vals * np.repeat(np.exp2(scales.astype(np.float64) - 127.0), 8, axis=1)[..., None]
    return vals.transpose(0, 1, 3, 2).reshape(g * 512, n)


D, E, T, I, Q = 512, 512, 2048, 512, 128


def setup_inputs():
    n = np.random.standard_normal
    idx2 = np.random.permutation(I)[:I]
    idx = np.random.permutation(T)[:I]
    fd = mx_kscale(D)
    fe = mx_kscale(E)
    keysp = pack_weight(n((D, T)) / fd[:, None], "e4m3")
    valsp = pack_weight(n((E, T)) / fe[:, None], "e4m3")
    return {
        "query": (n((D, Q)) * 0.7 / np.sqrt(D) * fd[:, None]).astype(np.float32),
        "keys_words": keysp[0],
        "keys_scales": keysp[1],
        "gout": (n((E, Q)) * 1 / np.sqrt(E) * fe[:, None]).astype(np.float32),
        "vals_words": valsp[0],
        "vals_scales": valsp[1],
        "old": (0.5 * n((Q, T))).astype(np.float32),
        "offs2": striped(idx2),
        "offs": striped(idx),
    }


def reference(query, keys_words, keys_scales, gout, vals_words, vals_scales, old, offs2, offs):
    idx2 = unstriped(offs2)
    idx = unstriped(offs)
    keysu = unpack_weight(keys_words, keys_scales, "e4m3")
    valsu = unpack_weight(vals_words, vals_scales, "e4m3")
    queryq = mxq(f64(query), 0, "e4m3")
    keysidxg = keysu[:, idx]
    a = queryq.T @ keysidxg
    pa = np.exp(a)
    pb = np.sqrt(pa)
    p = pa * pb[:, idx2]
    z = np.sum(p, axis=1, keepdims=True)
    goutq = mxq(f64(gout), 0, "e4m3")
    valsidxg = valsu[:, idx]
    c0 = goutq.T @ valsidxg
    dz = np.sum(c0 * p / np.square(z) * (-1.0), axis=1, keepdims=True)
    dp = c0 / z + dz
    e1 = dp * pa
    s1 = np.zeros((Q, I))
    s1[:, idx2] = e1
    dpa = dp * pb[:, idx2] + s1 * 0.5 / np.sqrt(pa)
    da = dpa * pa
    gs = da * 512.0
    gf = np.zeros((Q, T))
    gf[:, idx] = gs
    y = f64(old) + gf
    return y

@@ -1,0 +1,176 @@
+from contextlib import ExitStack
+
+import concourse.mybir as mybir
+
+D, E, T, I, Q = 512, 512, 2048, 512, 128
+FLOPS = 2 * Q * I * (D + E)
+
+F32 = mybir.dt.float32
+BF16 = mybir.dt.bfloat16
+I32 = mybir.dt.int32
+U32 = mybir.dt.uint32
+U16 = mybir.dt.uint16
+U8 = mybir.dt.uint8
+FP8X4 = mybir.dt.float8_e4m3fn_x4
+ALU = mybir.AluOpType
+ACT = mybir.ActivationFunctionType
+
+P = 128
+PACK = 4
+HALF = I // 2
+PB_COLS = I + 16
+LINK_COLS = 704
+OUT_CHUNKS = (512, 512, 512, 256, 256)
+
+
+def tile_attend_blinkedproduct_s_kernel(
+    tc, query, keys_words, keys_scales, gout, vals_words, vals_scales, old, offs2, offs, out
+):
+    nc = tc.nc
+    with ExitStack() as ctx:
+        lists = ctx.enter_context(tc.tile_pool(name="lists", bufs=1))
+        sb = ctx.enter_context(tc.tile_pool(name="sb", bufs=1))
+        ps = ctx.enter_context(tc.psum_pool(name="ps", bufs=1))
+
+        offs_t = lists.tile([P, I // 16], U16, name="offs_t")
+        offs2_t = lists.tile([P, I // 16], U16, name="offs2_t")
+        ks_pool = sb.tile([P, T], U8, name="ks_pool")
+        vs_pool = sb.tile([P, T], U8, name="vs_pool")
+        pb = sb.tile([P, PB_COLS], F32, name="pb")
+        gf = sb.tile([P, T], F32, name="gf")
+
+        nc.vector.memset(ks_pool[:].bitcast(I32), 0)
+        nc.vector.memset(pb[:, I:PB_COLS], 0.0)
+        nc.vector.memset(vs_pool[:].bitcast(I32), 0)
+        neg_half = sb.tile([P, 1], F32, name="neg_half", tag="factor_then_vw0", align_bytes=64)
+        nc.vector.memset(neg_half[:], -0.5)
+        nc.vector.memset(gf[:], 0.0)
+        warm = sb.tile([P, 1], F32, name="warm")
+        nc.scalar.activation(warm[:], pb[:, I : I + 1], ACT.Exp)
+
+        def load_scales(queue, pool_tile, scales):
+            for quad in range(4):
+                queue.dma_start(
+                    out=pool_tile[32 * quad : 32 * quad + 4, :].bitcast(I32),
+                    in_=scales[0, 4 * quad : 4 * quad + 4, :].bitcast(I32),
+                )
+
+        def load_words(pool_tile, words):
+            nc.sync.dma_start(out=pool_tile[:], in_=words[0].rearrange("p n t -> p (n t)").bitcast(I32))
+
+        def load_rows(raw, rows):
+            nc.sync.dma_start(out=raw[:], in_=rows.rearrange("(p j) w -> p j w", j=PACK))
+
+        def interleave(name, raw):
+            grouped = sb.tile([P, Q, PACK], BF16, name=name, align_bytes=64)
+            nc.scalar.copy(out=grouped[:], in_=raw[:].rearrange("p j w -> p w j"))
+            return grouped
+
+        def quantize(name, grouped):
+            codes = sb.tile([P, Q], U32, name=name + "_codes", align_bytes=64)
+            scales = sb.tile([P, Q], U8, name=name + "_scales", align_bytes=64)
+            nc.vector.quantize_mx(
+                out=codes[:].bitcast(FP8X4), scales=scales[:], in_=grouped[:].rearrange("p w j -> p (w j)")
+            )
+            return codes, scales
+
+        def gather_scales(name, pool_tile):
+            picked = sb.tile([P, I], U8, name=name, align_bytes=64)
+            nc.vector.tensor_copy(picked[:], pool_tile[:].indirect(offs_t[:]))
+            return picked
+
+        def gather_words(tags, pool_tile):
+            halves = []
+            for h in range(2):
+                picked = sb.tile([P, HALF], U32, name=tags[h], align_bytes=64)
+                nc.vector.tensor_copy(
+                    picked[:], pool_tile[:].bitcast(U32).indirect(offs_t[:, h * HALF // 16 : (h + 1) * HALF // 16])
+                )
+                halves.append(picked)
+            return halves
+
+        def multiply(name, halves, picked_scales, codes, scales):
+            acc = ps.tile([P, I], F32, name=name)
+            for h in range(2):
+                cols = slice(h * HALF, (h + 1) * HALF)
+                nc.tensor.matmul_mx(
+                    out=acc[:, cols],
+                    lhsT=codes[:].bitcast(FP8X4),
+                    lhsT_scale=scales[:],
+                    rhs=halves[h][:].bitcast(FP8X4),
+                    rhs_scale=picked_scales[:, cols],
+                    start=True,
+                    stop=True,
+                )
+            return acc
+
+        q_raw = sb.tile([P, PACK, Q], F32, name="q_raw")
+        g_raw = sb.tile([P, PACK, Q], F32, name="g_raw", tag="g_then_half_a")
+        kw_pool = sb.tile([P, T], I32, name="kw_pool", tag="keys_then_old")
+        vw_pool = sb.tile([P, T], I32, name="vw_pool", tag="vals_then_p")
+        nc.sync.dma_start(offs_t[:], offs)
+        load_rows(q_raw, query)
+        load_scales(nc.sync, ks_pool, keys_scales)
+        load_words(kw_pool, keys_words)
+        nc.sync.dma_start(offs2_t[:], offs2)
+        load_scales(nc.sync, vs_pool, vals_scales)
+        load_rows(g_raw, gout)
+        load_words(vw_pool, vals_words)
+
+        ks = gather_scales("ks", ks_pool)
+        q_codes, q_scales = quantize("q", interleave("q_bf", q_raw))
+        kw = gather_words(("kw0", "kw1"), kw_pool)
+        a = multiply("a", kw, ks, q_codes, q_scales)
+        old_t = sb.tile([P, T], F32, name="old_t", tag="keys_then_old")
+        nc.sync.dma_start(old_t[:], old)
+        vs = gather_scales("vs", vs_pool)
+        g_bf = interleave("g_bf", g_raw)
+
+        neg_half_a = sb.tile([P, I], F32, name="neg_half_a", tag="g_then_half_a")
+        shift = sb.tile([P, 1], F32, name="shift")
+        nc.vector.tensor_scalar(neg_half_a[:], a[:], neg_half[:], None, ALU.mult, ALU.min, accum_out=shift[:])
+        nc.scalar.activation(pb[:, 0:I], neg_half_a[:], ACT.Exp, bias=shift[:], scale=-1.0)
+        pa = [sb.tile([P, HALF], F32, name="pa%d" % h) for h in range(2)]
+        for h in range(2):
+            nc.scalar.activation(pa[h][:], pb[:, h * HALF : (h + 1) * HALF], ACT.Square)
+
+        g_codes, g_scales = quantize("g", g_bf)
+        vw = gather_words(("factor_then_vw0", "vw1"), vw_pool)
+        c0 = multiply("c0", vw, vs, g_codes, g_scales)
+
+        p = sb.tile([P, I], F32, name="p", tag="vals_then_p")
+        for h in range(2):
+            nc.vector.tensor_tensor(
+                p[:, h * HALF : (h + 1) * HALF],
+                pb[:].indirect(offs2_t[:, h * HALF // 16 : (h + 1) * HALF // 16]),
+                pa[h][:],
+                ALU.mult,
+            )
+
+        p_scaled = sb.tile([P, I], F32, name="p_scaled")
+        z_scaled = sb.tile([P, 1], F32, name="z_scaled")
+        nc.scalar.activation(p_scaled[:], p[:], ACT.Copy, scale=1.0 / 256.0, accum_out=z_scaled[:])
+        cp = sb.tile([P, I], F32, name="cp")
+        cp_sum = sb.tile([P, 1], F32, name="cp_sum")
+        nc.vector.scalar_tensor_tensor(cp[:], c0[:], 1.0, p[:], ALU.mult, ALU.mult, accum_out=cp_sum[:])
+        row_scale = sb.tile([P, 1], F32, name="row_scale")
+        nc.vector.reciprocal(row_scale[:], z_scaled[:])
+        mean_c0 = sb.tile([P, 1], F32, name="mean_c0")
+        nc.vector.tensor_scalar(mean_c0[:], cp_sum[:], row_scale[:], 1.0 / 256.0, ALU.mult, ALU.mult)
+        w = sb.tile([P, I], F32, name="w")
+        nc.vector.scalar_tensor_tensor(w[:], c0[:], mean_c0[:], p[:], ALU.subtract, ALU.mult)
+
+        linked = sb.tile([P, LINK_COLS], F32, name="linked")
+        nc.vector.tensor_copy(linked[:].indirect(offs2_t[:]), w[:])
+        w2 = sb.tile([P, I], F32, name="w2")
+        nc.scalar.activation(w2[:], w[:], ACT.Copy, scale=2.0)
+        nc.vector.tensor_tensor(gf[:].indirect(offs_t[:]), linked[:, 0:I], w2[:], ALU.add)
+
+        start = 0
+        for n, width in enumerate(OUT_CHUNKS):
+            cols = slice(start, start + width)
+            res = sb.tile([P, width], F32, name="res%d" % n)
+            nc.vector.scalar_tensor_tensor(res[:], gf[:, cols], row_scale[:], old_t[:, cols], ALU.mult, ALU.add)
+            queue = nc.sync if n % 2 == 0 else nc.scalar
+            queue.dma_start(out=out[:, cols], in_=res[:])
+            start = start + width

@@ -45,8 +45,6 @@ def tile_attend_blinkedproduct_s_kernel(
         neg_half = sb.tile([P, 1], F32, name="neg_half", tag="factor_then_vw0", align_bytes=64)
         nc.vector.memset(neg_half[:], -0.5)
         nc.vector.memset(gf[:], 0.0)
-        warm = sb.tile([P, 1], F32, name="warm")
-        nc.scalar.activation(warm[:], pb[:, I : I + 1], ACT.Exp)
 
         def load_scales(queue, pool_tile, scales):
             for quad in range(4):

from contextlib import ExitStack

import concourse.mybir as mybir

D, E, T, I, Q = 512, 512, 2048, 512, 128
FLOPS = 2 * Q * I * (D + E)

F32 = mybir.dt.float32
BF16 = mybir.dt.bfloat16
I32 = mybir.dt.int32
U32 = mybir.dt.uint32
U16 = mybir.dt.uint16
U8 = mybir.dt.uint8
FP8X4 = mybir.dt.float8_e4m3fn_x4
ALU = mybir.AluOpType
ACT = mybir.ActivationFunctionType

P = 128
PACK = 4
HALF = I // 2
PB_COLS = I + 16
LINK_COLS = 704
OUT_CHUNKS = (512, 512, 512, 256, 256)


def tile_attend_blinkedproduct_s_kernel(
    tc, query, keys_words, keys_scales, gout, vals_words, vals_scales, old, offs2, offs, out
):
    nc = tc.nc
    with ExitStack() as ctx:
        lists = ctx.enter_context(tc.tile_pool(name="lists", bufs=1))
        sb = ctx.enter_context(tc.tile_pool(name="sb", bufs=1))
        ps = ctx.enter_context(tc.psum_pool(name="ps", bufs=1))

        offs_t = lists.tile([P, I // 16], U16, name="offs_t")
        offs2_t = lists.tile([P, I // 16], U16, name="offs2_t")
        ks_pool = sb.tile([P, T], U8, name="ks_pool")
        vs_pool = sb.tile([P, T], U8, name="vs_pool")
        pb = sb.tile([P, PB_COLS], F32, name="pb")
        gf = sb.tile([P, T], F32, name="gf")

        nc.vector.memset(ks_pool[:].bitcast(I32), 0)
        nc.vector.memset(pb[:, I:PB_COLS], 0.0)
        nc.vector.memset(vs_pool[:].bitcast(I32), 0)
        neg_half = sb.tile([P, 1], F32, name="neg_half", tag="factor_then_vw0", align_bytes=64)
        nc.vector.memset(neg_half[:], -0.5)
        nc.vector.memset(gf[:], 0.0)

        def load_scales(queue, pool_tile, scales):
            for quad in range(4):
                queue.dma_start(
                    out=pool_tile[32 * quad : 32 * quad + 4, :].bitcast(I32),
                    in_=scales[0, 4 * quad : 4 * quad + 4, :].bitcast(I32),
                )

        def load_words(pool_tile, words):
            nc.sync.dma_start(out=pool_tile[:], in_=words[0].rearrange("p n t -> p (n t)").bitcast(I32))

        def load_rows(raw, rows):
            nc.sync.dma_start(out=raw[:], in_=rows.rearrange("(p j) w -> p j w", j=PACK))

        def interleave(name, raw):
            grouped = sb.tile([P, Q, PACK], BF16, name=name, align_bytes=64)
            nc.scalar.copy(out=grouped[:], in_=raw[:].rearrange("p j w -> p w j"))
            return grouped

        def quantize(name, grouped):
            codes = sb.tile([P, Q], U32, name=name + "_codes", align_bytes=64)
            scales = sb.tile([P, Q], U8, name=name + "_scales", align_bytes=64)
            nc.vector.quantize_mx(
                out=codes[:].bitcast(FP8X4), scales=scales[:], in_=grouped[:].rearrange("p w j -> p (w j)")
            )
            return codes, scales

        def gather_scales(name, pool_tile):
            picked = sb.tile([P, I], U8, name=name, align_bytes=64)
            nc.vector.tensor_copy(picked[:], pool_tile[:].indirect(offs_t[:]))
            return picked

        def gather_words(tags, pool_tile):
            halves = []
            for h in range(2):
                picked = sb.tile([P, HALF], U32, name=tags[h], align_bytes=64)
                nc.vector.tensor_copy(
                    picked[:], pool_tile[:].bitcast(U32).indirect(offs_t[:, h * HALF // 16 : (h + 1) * HALF // 16])
                )
                halves.append(picked)
            return halves

        def multiply(name, halves, picked_scales, codes, scales):
            acc = ps.tile([P, I], F32, name=name)
            for h in range(2):
                cols = slice(h * HALF, (h + 1) * HALF)
                nc.tensor.matmul_mx(
                    out=acc[:, cols],
                    lhsT=codes[:].bitcast(FP8X4),
                    lhsT_scale=scales[:],
                    rhs=halves[h][:].bitcast(FP8X4),
                    rhs_scale=picked_scales[:, cols],
                    start=True,
                    stop=True,
                )
            return acc

        q_raw = sb.tile([P, PACK, Q], F32, name="q_raw")
        g_raw = sb.tile([P, PACK, Q], F32, name="g_raw", tag="g_then_half_a")
        kw_pool = sb.tile([P, T], I32, name="kw_pool", tag="keys_then_old")
        vw_pool = sb.tile([P, T], I32, name="vw_pool", tag="vals_then_p")
        nc.sync.dma_start(offs_t[:], offs)
        load_rows(q_raw, query)
        load_scales(nc.sync, ks_pool, keys_scales)
        load_words(kw_pool, keys_words)
        nc.sync.dma_start(offs2_t[:], offs2)
        load_scales(nc.sync, vs_pool, vals_scales)
        load_rows(g_raw, gout)
        load_words(vw_pool, vals_words)

        ks = gather_scales("ks", ks_pool)
        q_codes, q_scales = quantize("q", interleave("q_bf", q_raw))
        kw = gather_words(("kw0", "kw1"), kw_pool)
        a = multiply("a", kw, ks, q_codes, q_scales)
        old_t = sb.tile([P, T], F32, name="old_t", tag="keys_then_old")
        nc.sync.dma_start(old_t[:], old)
        vs = gather_scales("vs", vs_pool)
        g_bf = interleave("g_bf", g_raw)

        neg_half_a = sb.tile([P, I], F32, name="neg_half_a", tag="g_then_half_a")
        shift = sb.tile([P, 1], F32, name="shift")
        nc.vector.tensor_scalar(neg_half_a[:], a[:], neg_half[:], None, ALU.mult, ALU.min, accum_out=shift[:])
        nc.scalar.activation(pb[:, 0:I], neg_half_a[:], ACT.Exp, bias=shift[:], scale=-1.0)
        pa = [sb.tile([P, HALF], F32, name="pa%d" % h) for h in range(2)]
        for h in range(2):
            nc.scalar.activation(pa[h][:], pb[:, h * HALF : (h + 1) * HALF], ACT.Square)

        g_codes, g_scales = quantize("g", g_bf)
        vw = gather_words(("factor_then_vw0", "vw1"), vw_pool)
        c0 = multiply("c0", vw, vs, g_codes, g_scales)

        p = sb.tile([P, I], F32, name="p", tag="vals_then_p")
        for h in range(2):
            nc.vector.tensor_tensor(
                p[:, h * HALF : (h + 1) * HALF],
                pb[:].indirect(offs2_t[:, h * HALF // 16 : (h + 1) * HALF // 16]),
                pa[h][:],
                ALU.mult,
            )

        p_scaled = sb.tile([P, I], F32, name="p_scaled")
        z_scaled = sb.tile([P, 1], F32, name="z_scaled")
        nc.scalar.activation(p_scaled[:], p[:], ACT.Copy, scale=1.0 / 256.0, accum_out=z_scaled[:])
        cp = sb.tile([P, I], F32, name="cp")
        cp_sum = sb.tile([P, 1], F32, name="cp_sum")
        nc.vector.scalar_tensor_tensor(cp[:], c0[:], 1.0, p[:], ALU.mult, ALU.mult, accum_out=cp_sum[:])
        row_scale = sb.tile([P, 1], F32, name="row_scale")
        nc.vector.reciprocal(row_scale[:], z_scaled[:])
        mean_c0 = sb.tile([P, 1], F32, name="mean_c0")
        nc.vector.tensor_scalar(mean_c0[:], cp_sum[:], row_scale[:], 1.0 / 256.0, ALU.mult, ALU.mult)
        w = sb.tile([P, I], F32, name="w")
        nc.vector.scalar_tensor_tensor(w[:], c0[:], mean_c0[:], p[:], ALU.subtract, ALU.mult)

        linked = sb.tile([P, LINK_COLS], F32, name="linked")
        nc.vector.tensor_copy(linked[:].indirect(offs2_t[:]), w[:])
        w2 = sb.tile([P, I], F32, name="w2")
        nc.scalar.activation(w2[:], w[:], ACT.Copy, scale=2.0)
        nc.vector.tensor_tensor(gf[:].indirect(offs_t[:]), linked[:, 0:I], w2[:], ALU.add)

        start = 0
        for n, width in enumerate(OUT_CHUNKS):
            cols = slice(start, start + width)
            res = sb.tile([P, width], F32, name="res%d" % n)
            nc.vector.scalar_tensor_tensor(res[:], gf[:, cols], row_scale[:], old_t[:, cols], ALU.mult, ALU.add)
            queue = nc.sync if n % 2 == 0 else nc.scalar
            queue.dma_start(out=out[:, cols], in_=res[:])
            start = start + width
